import numpy as np
import ml_dtypes


def mxq(x, axis, fmt="e4m3"):
    dtype, down = {"e4m3": (ml_dtypes.float8_e4m3fn, 7), "e5m2": (ml_dtypes.float8_e5m2, 14)}[fmt]
    v = np.moveaxis(np.asarray(x, np.float32).astype(ml_dtypes.bfloat16).astype(np.float64), axis, -1)
    blocks = v.reshape(v.shape[:-1] + (-1, 32))
    amax = np.abs(blocks).max(-1, keepdims=True)
    byte = np.maximum(np.where(amax > 0, np.frexp(amax)[1] - 1 + 127, 0) - down, 1)
    scale = np.exp2(byte - 127.0)
    codes = (blocks / scale).astype(np.float32).astype(dtype).astype(np.float64)
    return np.moveaxis((codes * scale).reshape(v.shape), -1, axis)


WIDE = False


def mx_kscale(k):
    if not WIDE:
        return np.ones(k)
    levels = np.array([10, -10, 5, -5, 0])
    if k % 512:
        return np.exp2(np.random.permutation(np.resize(levels, k // 32))).repeat(32)
    a = np.empty((k // 512, 16))
    for p in range(k // 512):
        a[p, :8] = np.random.permutation(np.resize(levels, 8))
        for g in range(8):
            far = levels[np.abs(levels - a[p, g]) >= 10]
            a[p, g + 8] = far[np.random.randint(len(far))]
    return np.exp2(a.ravel()).repeat(32)


BF16 = ml_dtypes.bfloat16


def bf(x):
    return np.asarray(x, np.float32).astype(BF16)


def f64(x):
    return np.asarray(x).astype(np.float64)


E2M1 = np.array([0.0, 0.5, 1.0, 1.5, 2.0, 3.0, 4.0, 6.0, -0.0, -0.5, -1.0, -1.5, -2.0, -3.0, -4.0, -6.0])


def pack_weight(w, fmt):
    k, n = w.shape
    w = f64(bf(w)).reshape(k // 32, 32, n)
    amax = np.abs(w).max(1)
    if fmt == "e4m3":
        byte = np.frexp(amax)[1] - 1 + 127 - 7
    else:
        mant, ex = np.frexp(amax / 6.0)
        byte = np.where(mant > 0.5, ex, ex - 1) + 127
    byte = np.clip(np.where(amax > 0, byte, 1), 1, 254)
    scaled = (w * np.exp2(127.0 - byte)[:, None, :]).reshape(k, n).astype(np.float32)
    by_word = np.ascontiguousarray(scaled.reshape(k // 512, 128, 4, n).transpose(0, 1, 3, 2))
    if fmt == "e4m3":
        words = by_word.astype(ml_dtypes.float8_e4m3fn).view(np.uint8)
    else:
        c = by_word.astype(ml_dtypes.float4_e2m1fn).view(np.uint8) & 0xF
        words = c[..., 0::2] | (c[..., 1::2] << 4)
    return np.ascontiguousarray(words), np.ascontiguousarray(byte.astype(np.uint8).reshape(k // 512, 16, n))


def unpack_weight(words, scales, fmt):
    g, p, n, _ = words.shape
    if fmt == "e4m3":
        vals = np.ascontiguousarray(words).view(ml_dtypes.float8_e4m3fn).astype(np.float64)
    else:
        nib = np.empty((g, p, n, 4), np.uint8)
        nib[..., 0::2] = words & 0xF
        nib[..., 1::2] = words >> 4
        vals = E2M1[nib]
    vals = vals * np.repeat(np.exp2(scales.astype(np.float64) - 127.0), 8, axis=1)[..., None]
    return vals.transpose(0, 1, 3, 2).reshape(g * 512, n)
def pack4(w):
    words, scales = pack_weight(w, "e2m1")
    return words.reshape(words.shape[0], 128, -1), scales


def unpack4(words, scales):
    return unpack_weight(words.reshape(words.shape[0], 128, -1, 2), scales, "e2m1")


E4M3FN = np.array([(-1.0 if i & 128 else 1.0) * ((1.0 + (i & 7) / 8.0) * 2.0 ** (((i >> 3) & 15) - 7) if i & 120 else (i & 7) * 2.0 ** -9) for i in range(256)])


def e4m3fn_bytes(y):
    return np.clip(np.asarray(y, np.float64), -448.0, 448.0).astype(np.float32).astype(ml_dtypes.float8_e4m3fn).view(np.uint8)


def e4m3fn_values(b):
    return E4M3FN[b]

def planes(Y):
    n, m = Y.shape
    b = f64(bf(Y)).reshape(n // 32, 32, m)
    amax = np.abs(b).max(1)
    byte = np.clip(np.where(amax > 0, np.frexp(amax)[1] - 1 + 127 - 7, 1), 1, 254)
    codes = (b * np.exp2(127.0 - byte)[:, None, :]).reshape(n, m).astype(np.float32).astype(ml_dtypes.float8_e4m3fn).view(np.uint8)
    words = codes.reshape(n // 512, 128, 4, m).transpose(0, 1, 3, 2)
    return np.ascontiguousarray(words), np.ascontiguousarray(byte.astype(np.uint8).reshape(n // 512, 16, m))


T, D, F, B = 512, 1024, 2048, 128

def setup_inputs():
    s, t = mx_kscale(D), mx_kscale(F)
    XT = np.random.randn(D, T) * s[:, None]
    Wg = np.random.randn(D, F) / np.sqrt(D) / s[:, None]
    Wu = np.random.randn(D, F) / np.sqrt(D) / s[:, None] * t[None, :]
    Wd = 1.5 * np.random.randn(F, D) / np.sqrt(F) / t[:, None]
    Wd_scale = np.float32(np.abs(Wd).reshape(F // B, B, D // B, B).max(axis=(1, 3)) / 448.0)
    Wd_bytes = e4m3fn_bytes(Wd / np.repeat(np.repeat(f64(Wd_scale), B, axis=0), B, axis=1))
    XT_words, XT_scales = pack4(XT)
    Wg_words, Wg_scales = pack4(Wg)
    Wu_words, Wu_scales = pack4(Wu)
    c = np.exp(0.8 * np.random.randn(D))
    return {"XT_words": XT_words, "XT_scales": XT_scales,
            "Wg_words": Wg_words, "Wg_scales": Wg_scales,
            "Wu_words": Wu_words, "Wu_scales": Wu_scales,
            "Wd_bytes": Wd_bytes, "Wd_scale": Wd_scale,
            "bg": bf(0.3 * np.random.randn(F)),
            "gain": bf(c * (1 + 0.1 * np.random.randn(D))),
            "res": bf(0.5 * c[None, :] * np.random.randn(T, D))}

def reference(XT_words, XT_scales, Wg_words, Wg_scales, Wu_words, Wu_scales, Wd_bytes, Wd_scale, bg, gain, res):
    XT = unpack4(XT_words, XT_scales)
    Wg = unpack4(Wg_words, Wg_scales)
    Wu = unpack4(Wu_words, Wu_scales)
    a = (XT.T @ Wg) + f64(bg)
    b = XT.T @ Wu
    h = b / (1.0 + np.exp(-a))
    Wd = e4m3fn_values(Wd_bytes) * np.repeat(np.repeat(f64(Wd_scale), B, axis=0), B, axis=1)
    o = mxq(h, 1, "e4m3") @ mxq(Wd, 0, "e4m3")
    y = f64(res) + f64(gain) * o
    Y = y.T
    words, scales = planes(Y)
    return y, words, scales

@@ -1,0 +1,367 @@
+from contextlib import ExitStack
+
+import concourse.mybir as mybir
+from concourse.masks import make_identity
+
+T, D, F = 512, 1024, 2048
+FLOPS = 2 * T * D * F * 3
+
+F32 = mybir.dt.float32
+BF16 = mybir.dt.bfloat16
+I32 = mybir.dt.int32
+U32 = mybir.dt.uint32
+U8 = mybir.dt.uint8
+FP8 = mybir.dt.float8_e4m3fn
+FP8X4 = mybir.dt.float8_e4m3fn_x4
+FP4X4 = mybir.dt.float4_e2m1fn_x4
+ACT = mybir.ActivationFunctionType
+ALU = mybir.AluOpType
+
+P = 128
+PACK = 4
+KP = P * PACK
+DG = D // KP
+FG = F // KP
+FT = F // P
+TT = T // P
+HS = [(), (1,), (1,), (1,)]
+WS = [(), (), (), ()]
+YV = [False, False, True, True]
+
+
+def tile_fp4_sigmoid_glu_ffn_b16_kernel(
+    tc, XT_words, XT_scales, Wg_words, Wg_scales, Wu_words, Wu_scales,
+    Wd_bytes, Wd_scale, bg, gain, res, out_0, out_1, out_2,
+):
+    nc = tc.nc
+    with ExitStack() as ctx:
+        keep = ctx.enter_context(tc.tile_pool(name="keep", bufs=1))
+        work = ctx.enter_context(tc.tile_pool(name="work", bufs=2))
+        psum = ctx.enter_context(tc.psum_pool(name="psum", bufs=1))
+        ctx.enter_context(tc.manual_schedule(engines={mybir.EngineType.SP}))
+
+        def kept(name, shape, dtype):
+            return keep.tile(shape, dtype, name=name, align_bytes=64)
+
+        def bank(b, shape=(P, KP), dtype=F32):
+            return psum.tile(list(shape), dtype, name="bank%d" % b, tag="bank%d" % b)
+
+        wd_bytes = {}
+        for g in range(FG):
+            for u in range(2):
+                wd_bytes[g, u] = kept("wd_bytes%d_%d" % (g, u), [P, 2 * D], U8)
+        x_words = kept("x_words", [P, DG, 2 * T], U8)
+        x_scales = kept("x_scales", [P, DG, T], U8)
+        wg_words = [kept("wg_words%d" % g, [P, DG, 2 * KP], U8) for g in range(FG)]
+        wu_words = [kept("wu_words%d" % g, [P, DG, 2 * KP], U8) for g in range(FG)]
+        wg_scales = [kept("wg_scales0", [P, DG, KP], U8), kept("wg_scales1", [P, DG, F - KP], U8)]
+        wu_scales = [kept("wu_scales0", [P, DG, KP], U8), kept("wu_scales1", [P, DG, F - KP], U8)]
+        table = kept("table", [P, F // P * 8], F32)
+        wd_scale = kept("wd_scale", [P, FG, 8], F32)
+        bg_rows = kept("bg_rows", [P, P], BF16)
+        bias = kept("bias", [P, FT], F32)
+        gain_sb = kept("gain_sb", [P, DG, 16], BF16)
+        ident = kept("ident", [P, P], F32)
+        ident_bf = kept("ident_bf", [P, P], BF16)
+        warm = kept("warm", [P, 8], F32)
+        res_sb = [kept("res_sb%d" % m, [P, D], BF16) for m in range(TT)]
+        res_t = kept("res_t", [P, DG, 2, T], F32)
+        wd_codes = {}
+        wd_mx = {}
+        for g in range(FG):
+            for n in range(DG):
+                wd_codes[g, n] = kept("wd_codes%d_%d" % (g, n), [P, KP], U32)
+                wd_mx[g, n] = kept("wd_mx%d_%d" % (g, n), [P, KP], U8)
+        h_nat = [kept("h_nat%d" % g, [P, PACK, T], BF16) for g in range(FG)]
+        h_back = [kept("h_back%d" % g, [P, PACK, T], BF16) for g in range(FG)]
+        h_codes = [kept("h_codes%d" % g, [P, T], U32) for g in range(FG)]
+        h_mx = [kept("h_mx%d" % g, [P, T], U8) for g in range(FG)]
+        y_t = [kept("y_t%d" % n, [P, PACK, T], F32) for n in range(DG)]
+        y_grp = [kept("y_grp%d" % n, [P, T, PACK], BF16) for n in range(DG)]
+        y_codes = [kept("y_codes%d" % n, [P, T], U32) for n in range(DG)]
+        y_mx = [kept("y_mx%d" % n, [P, T], U8) for n in range(DG)]
+
+        def load_words(dst, src, g):
+            view = src.bitcast(I32).rearrange("d p w -> p d w")
+            width = dst.shape[2] // 4
+            nc.sync.dma_start(out=dst[:].bitcast(I32), in_=view[:, :, width * g : width * (g + 1)])
+
+        def load_scales(dst, src, first=0):
+            cols = slice(first // 4, (first + dst.shape[2]) // 4)
+            for q in range(4):
+                nc.sync.dma_start(
+                    out=dst[32 * q : 32 * q + 4].bitcast(I32),
+                    in_=src.bitcast(I32)[:, 4 * q : 4 * q + 4, cols].rearrange("d r w -> r d w"),
+                )
+
+        def load_wd(g, halves=(0, 1)):
+            rows = Wd_bytes.rearrange("(g p u e) n -> g u p (e n)", p=P, u=2, e=2)
+            for u in halves:
+                nc.sync.dma_start(out=wd_bytes[g, u][:], in_=rows[g, u])
+
+        nc.vector.memset(warm[:], 0.0)
+        nc.scalar.activation(out=warm[:, 4:5], in_=warm[:, 0:1], func=ACT.Sigmoid)
+        nc.vector.memset(bg_rows[:], 0.0)
+        for plane in (x_scales, wg_scales[0], wu_scales[0], wg_scales[1], wu_scales[1]):
+            nc.vector.memset(plane[:].bitcast(I32), 0)
+        make_identity(nc, ident[:])
+
+        load_wd(0, (0,))
+        nc.sync.dma_start(out=table[:], in_=Wd_scale.rearrange("i j -> (i j)").partition_broadcast(P))
+        load_wd(0, (1,))
+        load_scales(x_scales, XT_scales)
+        nc.sync.dma_start(out=bg_rows[0:FT, :], in_=bg.rearrange("(i p) -> i p", p=P))
+        load_words(x_words, XT_words, 0)
+        load_wd(1, (0,))
+        load_words(wg_words[0], Wg_words, 0)
+        load_scales(wg_scales[0], Wg_scales)
+        load_wd(1, (1,))
+        load_words(wu_words[0], Wu_words, 0)
+        load_scales(wu_scales[0], Wu_scales)
+        load_wd(2)
+        load_scales(wg_scales[1], Wg_scales, KP)
+        load_scales(wu_scales[1], Wu_scales, KP)
+        load_words(wg_words[1], Wg_words, 1)
+        load_words(wu_words[1], Wu_words, 1)
+        load_wd(3)
+        for m in range(TT):
+            nc.sync.dma_start(out=res_sb[m][:], in_=res[P * m : P * (m + 1), :])
+        load_words(wg_words[2], Wg_words, 2)
+        load_words(wu_words[2], Wu_words, 2)
+        load_words(wg_words[3], Wg_words, 3)
+        load_words(wu_words[3], Wu_words, 3)
+        nc.sync.dma_start(out=gain_sb[:, :, 0:PACK], in_=gain.rearrange("(n p t) -> p n t", p=P, t=PACK))
+
+        nc.vector.tensor_copy(out=ident_bf[:], in_=ident[:])
+        by_quadrant = table[:].rearrange("p (g q j) -> p q g j", g=FG, q=4)
+
+        def pick_scales():
+            for q in range(4):
+                nc.vector.tensor_copy(out=wd_scale[32 * q : 32 * q + 32], in_=by_quadrant[32 * q : 32 * q + 32, q])
+
+        bias_ps = bank(7, (P, P), BF16)
+        nc.tensor.transpose(bias_ps[:], bg_rows[:], ident_bf[:])
+
+        wide = {}
+        grouped = {}
+
+        def widen(g, n, t, on_vector=False):
+            if t == 0:
+                wide[g, n] = work.tile([P, PACK, KP], BF16, name="wide", bufs=6, align_bytes=64)
+            first = D * (t % 2) + KP * n
+            src = wd_bytes[g, t // 2][:, first : first + KP].bitcast(FP8)
+            if on_vector:
+                nc.vector.tensor_copy(out=wide[g, n][:, t, :], in_=src)
+            else:
+                nc.scalar.copy(out=wide[g, n][:, t, :], in_=src)
+
+        def scale_group(g, n, j, on_scalar=False):
+            if j == 0:
+                grouped[g, n] = work.tile([P, KP, PACK], BF16, name="grouped", bufs=4, align_bytes=64)
+            dst = grouped[g, n][:].rearrange("p (s m) t -> p s m t", s=PACK)[:, :, 32 * j : 32 * (j + 1), :]
+            src = wide[g, n][:, :, P * j : P * (j + 1)].rearrange("p t (m s) -> p s m t", s=PACK)
+            col = PACK * n + j
+            factor = wd_scale[:, g, col : col + 1]
+            if on_scalar:
+                nc.scalar.activation(out=dst, in_=src, func=ACT.Copy, scale=factor)
+            else:
+                nc.vector.tensor_scalar(out=dst, in0=src, scalar1=factor, scalar2=None, op0=ALU.mult)
+
+        def quant_wd(g, n):
+            nc.vector.quantize_mx(
+                out=wd_codes[g, n][:].bitcast(FP8X4), scales=wd_mx[g, n][:],
+                in_=grouped[g, n][:].rearrange("p c t -> p (c t)"),
+            )
+
+        acc = {}
+        sig = {}
+
+        def up_matmuls(i):
+            g, s = divmod(i, PACK)
+            col = P * i - KP * min(g, 1)
+            for name, words, scales, b in (("a", wg_words, wg_scales, i % 2), ("b", wu_words, wu_scales, 2 + i % 2)):
+                acc[name, i] = bank(b)
+                for d in range(DG):
+                    nc.tensor.matmul_mx(
+                        out=acc[name, i][:],
+                        lhsT=words[g][:, d, 2 * P * s : 2 * P * (s + 1)].bitcast(FP4X4),
+                        lhsT_scale=scales[min(g, 1)][:, d, col : col + P],
+                        rhs=x_words[:, d, :].bitcast(FP4X4), rhs_scale=x_scales[:, d, :],
+                        start=(d == 0), stop=(d == DG - 1),
+                    )
+
+        def sigmoid(i):
+            sig[i] = work.tile([P, T], F32, name="sig", bufs=3)
+            nc.scalar.activation(out=sig[i][:], in_=acc["a", i][:], func=ACT.Sigmoid, bias=bias[:, i : i + 1])
+
+        def gate(i):
+            g, s = divmod(i, PACK)
+            nc.vector.tensor_tensor(out=h_nat[g][:, s, :], in0=acc["b", i][:], in1=sig[i][:], op=ALU.mult)
+
+        park = out_0.bitcast(BF16).rearrange("r (t w) -> (r t) w", t=PACK)
+
+        def park_store(g, s0, s1):
+            rows = park[KP * g : KP * (g + 1), :].rearrange("(s p) w -> p s w", p=P)
+            nc.sync.dma_start(out=rows[:, s0:s1, :], in_=h_nat[g][:, s0:s1, :])
+
+        def park_load(g):
+            rows = park[KP * g : KP * (g + 1), :].rearrange("(p t) w -> p t w", t=PACK)
+            nc.sync.dma_start(out=h_back[g][:], in_=rows)
+
+        def shuffle(g, s):
+            for t in range(PACK):
+                nc.sync.dma_start(out=h_back[g][32 * s : 32 * (s + 1), t, :], in_=h_nat[g][t:P:PACK, s, :])
+
+        h_grp = {}
+
+        def group_h(g, half, on_scalar=False):
+            if half == 0:
+                h_grp[g] = work.tile([P, T, PACK], BF16, name="h_grp", bufs=4, align_bytes=64)
+            cols = slice(T // 2 * half, T // 2 * (half + 1))
+            dst = h_grp[g][:, cols, :].rearrange("p (c i) t -> p c t i", i=4)
+            src = h_back[g][:, :, cols].rearrange("p t (c i) -> p c t i", i=4)
+            if on_scalar:
+                nc.scalar.copy(out=dst, in_=src)
+            else:
+                nc.vector.tensor_copy(out=dst, in_=src)
+
+        def quant_h(g):
+            nc.vector.quantize_mx(
+                out=h_codes[g][:].bitcast(FP8X4), scales=h_mx[g][:],
+                in_=h_grp[g][:].rearrange("p c t -> p (c t)"),
+            )
+
+        res_ps = {}
+
+        def res_turn(m):
+            res_ps[m] = bank(4 + m, (P, DG, 2, P))
+            words = res_sb[m][:].bitcast(F32)
+            for n in range(DG):
+                for u in range(2):
+                    nc.tensor.transpose(res_ps[m][:, n, u, :], words[:, 256 * n + u : 256 * (n + 1) : 2], ident[:])
+
+        def res_copy(m):
+            nc.scalar.copy(out=res_t[:, :, :, P * m : P * (m + 1)], in_=res_ps[m][:])
+
+        o_ps = {}
+
+        passes = {0: 0, 1: 0}
+
+        def down_pass(n, g):
+            passes[n] = passes[n] + 1
+            for s in range(PACK):
+                if passes[n] == 1:
+                    o_ps[n, s] = bank(4 * (1 - n) + s)
+                nc.tensor.matmul_mx(
+                    out=o_ps[n, s][:],
+                    lhsT=wd_codes[g, n][:, P * s : P * (s + 1)].bitcast(FP8X4),
+                    lhsT_scale=wd_mx[g, n][:, P * s : P * (s + 1)],
+                    rhs=h_codes[g][:].bitcast(FP8X4), rhs_scale=h_mx[g][:],
+                    start=(passes[n] == 1), stop=(passes[n] == FG),
+                )
+
+        def finish(n, s, t0=0, t1=T):
+            u, e = divmod(s, 2)
+            res_cols = res_t[:, n, u, :].bitcast(BF16)[:, 2 * t0 + e : 2 * t1 : 2]
+            nc.vector.scalar_tensor_tensor(
+                out=y_t[n][:, s, t0:t1], in0=o_ps[n, s][:, t0:t1], scalar=gain_sb[:, n, s : s + 1], in1=res_cols,
+                op0=ALU.mult, op1=ALU.add,
+            )
+
+        y_ps = {}
+
+        def y_turn(n, m):
+            y_ps[n, m] = bank(4 + m, (P, PACK, P))
+            for s in range(PACK):
+                nc.tensor.transpose(y_ps[n, m][:, s, :], y_t[n][:, s, P * m : P * (m + 1)], ident[:])
+
+        def y_out(n, m, on_vector=False):
+            y_sb = work.tile([P, KP], F32, name="y_sb", bufs=8)
+            dst = y_sb[:].rearrange("r (p s) -> r p s", s=PACK)
+            src = y_ps[n, m][:].rearrange("r s p -> r p s")
+            if on_vector:
+                nc.vector.tensor_copy(out=dst, in_=src)
+            else:
+                nc.scalar.copy(out=dst, in_=src)
+            nc.sync.dma_start(out=out_0[P * m : P * (m + 1), KP * n : KP * (n + 1)], in_=y_sb[:])
+
+        def group_y(n, half, on_vector=False):
+            cols = slice(T // 2 * half, T // 2 * (half + 1))
+            dst = y_grp[n][:, cols, :].rearrange("p (c i) t -> p c t i", i=4)
+            src = y_t[n][:, :, cols].rearrange("p t (c i) -> p c t i", i=4)
+            if on_vector:
+                nc.vector.tensor_copy(out=dst, in_=src)
+            else:
+                nc.scalar.copy(out=dst, in_=src)
+
+        def quant_y(n, t0=0, t1=T):
+            nc.vector.quantize_mx(
+                out=y_codes[n][:, t0:t1].bitcast(FP8X4), scales=y_mx[n][:, t0:t1],
+                in_=y_grp[n][:, t0:t1, :].rearrange("p c t -> p (c t)"),
+            )
+            words = out_1[n].rearrange("p m t -> p (m t)").bitcast(I32)
+            nc.sync.dma_start(out=words[:, t0:t1], in_=y_codes[n][:, t0:t1].bitcast(I32))
+
+        def scales_out(n, queues):
+            for q in range(4):
+                queues[q % len(queues)].dma_start(
+                    out=out_2[n, 4 * q : 4 * q + 4, :].bitcast(I32), in_=y_mx[n][32 * q : 32 * q + 4, :].bitcast(I32)
+                )
+
+        nc.scalar.copy(out=bias[:], in_=bias_ps[:, 0:FT])
+        pick_scales()
+
+        def prepare_wd(g, n, widen_on_vector=(), group_on_scalar=()):
+            for t in range(PACK):
+                widen(g, n, t, t in widen_on_vector)
+            for j in range(PACK):
+                scale_group(g, n, j, j in group_on_scalar)
+            quant_wd(g, n)
+
+        def prepare_h(g, on_scalar=()):
+            group_h(g, 0, 0 in on_scalar)
+            group_h(g, 1, 1 in on_scalar)
+            quant_h(g)
+
+        for i in range(FT):
+            g, s = divmod(i, PACK)
+            up_matmuls(i)
+            sigmoid(i)
+            gate(i)
+            if g == FG - 1:
+                shuffle(g, s)
+            elif s % 2 == 1:
+                park_store(g, s - 1, s + 1)
+            if i in (7, 11, 13):
+                park_load((7, 11, 13).index(i))
+        prepare_wd(0, 0, (0, 2, 3))
+        for g in range(1, FG):
+            prepare_wd(g, 0)
+        for m in range(TT):
+            res_turn(m)
+            res_copy(m)
+        for g in range(FG):
+            prepare_h(g, HS[g])
+            down_pass(0, g)
+        half = T // 2
+        for s in range(PACK):
+            finish(0, s)
+        for m in range(TT):
+            y_turn(0, m)
+            y_out(0, m)
+        for g in range(FG):
+            prepare_wd(g, 1, (), WS[g])
+            down_pass(1, g)
+        group_y(0, 0, YV[0])
+        group_y(0, 1, YV[1])
+        quant_y(0)
+        scales_out(0, [nc.sync])
+        for h in range(2):
+            for s in range(PACK):
+                finish(1, s, half * h, half * (h + 1))
+            for m in (2 * h, 2 * h + 1):
+                y_turn(1, m)
+                y_out(1, m)
+            group_y(1, h, YV[2 + h])
+            quant_y(1, half * h, half * (h + 1))
+        scales_out(1, [nc.sync, nc.scalar])

@@ -24,9 +24,7 @@ DG = D // KP
 FG = F // KP
 FT = F // P
 TT = T // P
-HS = [(), (1,), (1,), (1,)]
-WS = [(), (), (), ()]
-YV = [False, False, True, True]
+RES_STEP = 9
 
 
 def tile_fp4_sigmoid_glu_ffn_b16_kernel(
@@ -38,7 +36,7 @@ def tile_fp4_sigmoid_glu_ffn_b16_kernel(
         keep = ctx.enter_context(tc.tile_pool(name="keep", bufs=1))
         work = ctx.enter_context(tc.tile_pool(name="work", bufs=2))
         psum = ctx.enter_context(tc.psum_pool(name="psum", bufs=1))
-        ctx.enter_context(tc.manual_schedule(engines={mybir.EngineType.SP}))
+        ctx.enter_context(tc.manual_schedule())
 
         def kept(name, shape, dtype):
             return keep.tile(shape, dtype, name=name, align_bytes=64)
@@ -118,19 +116,16 @@ def tile_fp4_sigmoid_glu_ffn_b16_kernel(
         load_wd(1, (1,))
         load_words(wu_words[0], Wu_words, 0)
         load_scales(wu_scales[0], Wu_scales)
-        load_wd(2)
         load_scales(wg_scales[1], Wg_scales, KP)
         load_scales(wu_scales[1], Wu_scales, KP)
-        load_words(wg_words[1], Wg_words, 1)
-        load_words(wu_words[1], Wu_words, 1)
-        load_wd(3)
+        for g in range(1, FG):
+            load_words(wg_words[g], Wg_words, g)
+            load_words(wu_words[g], Wu_words, g)
+            if g + 1 < FG:
+                load_wd(g + 1)
+        nc.sync.dma_start(out=gain_sb[:, :, 0:PACK], in_=gain.rearrange("(n p t) -> p n t", p=P, t=PACK))
         for m in range(TT):
             nc.sync.dma_start(out=res_sb[m][:], in_=res[P * m : P * (m + 1), :])
-        load_words(wg_words[2], Wg_words, 2)
-        load_words(wu_words[2], Wu_words, 2)
-        load_words(wg_words[3], Wg_words, 3)
-        load_words(wu_words[3], Wu_words, 3)
-        nc.sync.dma_start(out=gain_sb[:, :, 0:PACK], in_=gain.rearrange("(n p t) -> p n t", p=P, t=PACK))
 
         nc.vector.tensor_copy(out=ident_bf[:], in_=ident[:])
         by_quadrant = table[:].rearrange("p (g q j) -> p q g j", g=FG, q=4)
@@ -155,15 +150,17 @@ def tile_fp4_sigmoid_glu_ffn_b16_kernel(
             else:
                 nc.scalar.copy(out=wide[g, n][:, t, :], in_=src)
 
-        def scale_group(g, n, j, on_scalar=False):
+        def scale_group(g, n, j, on="V"):
             if j == 0:
                 grouped[g, n] = work.tile([P, KP, PACK], BF16, name="grouped", bufs=4, align_bytes=64)
-            dst = grouped[g, n][:].rearrange("p (s m) t -> p s m t", s=PACK)[:, :, 32 * j : 32 * (j + 1), :]
-            src = wide[g, n][:, :, P * j : P * (j + 1)].rearrange("p t (m s) -> p s m t", s=PACK)
+            dst = grouped[g, n][:].rearrange("p (s m) t -> p m t s", s=PACK)[:, 32 * j : 32 * (j + 1)]
+            src = wide[g, n][:, :, P * j : P * (j + 1)].rearrange("p t (m s) -> p m t s", s=PACK)
             col = PACK * n + j
             factor = wd_scale[:, g, col : col + 1]
-            if on_scalar:
+            if on == "S":
                 nc.scalar.activation(out=dst, in_=src, func=ACT.Copy, scale=factor)
+            elif on == "G":
+                nc.gpsimd.tensor_scalar(out=dst, in0=src, scalar1=factor, scalar2=0.0, op0=ALU.mult, op1=ALU.add)
             else:
                 nc.vector.tensor_scalar(out=dst, in0=src, scalar1=factor, scalar2=None, op0=ALU.mult)
 
@@ -212,18 +209,23 @@ def tile_fp4_sigmoid_glu_ffn_b16_kernel(
             for t in range(PACK):
                 nc.sync.dma_start(out=h_back[g][32 * s : 32 * (s + 1), t, :], in_=h_nat[g][t:P:PACK, s, :])
 
+        def move(dst, src, on):
+            if on == "S":
+                nc.scalar.copy(out=dst, in_=src)
+            elif on == "G":
+                nc.gpsimd.tensor_scalar(out=dst, in0=src, scalar1=1.0, scalar2=0.0, op0=ALU.mult, op1=ALU.add)
+            else:
+                nc.vector.tensor_copy(out=dst, in_=src)
+
         h_grp = {}
 
-        def group_h(g, half, on_scalar=False):
+        def group_h(g, half, on="V"):
             if half == 0:
                 h_grp[g] = work.tile([P, T, PACK], BF16, name="h_grp", bufs=4, align_bytes=64)
             cols = slice(T // 2 * half, T // 2 * (half + 1))
             dst = h_grp[g][:, cols, :].rearrange("p (c i) t -> p c t i", i=4)
             src = h_back[g][:, :, cols].rearrange("p t (c i) -> p c t i", i=4)
-            if on_scalar:
-                nc.scalar.copy(out=dst, in_=src)
-            else:
-                nc.vector.tensor_copy(out=dst, in_=src)
+            move(dst, src, on)
 
         def quant_h(g):
             nc.vector.quantize_mx(
@@ -285,14 +287,11 @@ def tile_fp4_sigmoid_glu_ffn_b16_kernel(
                 nc.scalar.copy(out=dst, in_=src)
             nc.sync.dma_start(out=out_0[P * m : P * (m + 1), KP * n : KP * (n + 1)], in_=y_sb[:])
 
-        def group_y(n, half, on_vector=False):
+        def group_y(n, half, on="S"):
             cols = slice(T // 2 * half, T // 2 * (half + 1))
             dst = y_grp[n][:, cols, :].rearrange("p (c i) t -> p c t i", i=4)
             src = y_t[n][:, :, cols].rearrange("p t (c i) -> p c t i", i=4)
-            if on_vector:
-                nc.vector.tensor_copy(out=dst, in_=src)
-            else:
-                nc.scalar.copy(out=dst, in_=src)
+            move(dst, src, on)
 
         def quant_y(n, t0=0, t1=T):
             nc.vector.quantize_mx(
@@ -308,60 +307,110 @@ def tile_fp4_sigmoid_glu_ffn_b16_kernel(
                     out=out_2[n, 4 * q : 4 * q + 4, :].bitcast(I32), in_=y_mx[n][32 * q : 32 * q + 4, :].bitcast(I32)
                 )
 
-        nc.scalar.copy(out=bias[:], in_=bias_ps[:, 0:FT])
+        blocks = [(0, 0), (0, 1), (1, 0), (1, 1), (2, 0), (3, 0), (2, 1), (3, 1)]
+
+        def group_pair(b, half, on="V"):
+            for j in range(2 * half, 2 * half + 2):
+                scale_group(*blocks[b], j, on)
+
+        widen(*blocks[0], 0, True)
+        widen(*blocks[0], 1)
         pick_scales()
+        widen(*blocks[0], 2, True)
+        widen(*blocks[0], 3, True)
+        for t in range(PACK):
+            widen(*blocks[1], t)
+        group_pair(0, 0)
+        group_pair(0, 1)
+        nc.scalar.copy(out=bias[:], in_=bias_ps[:, 0:FT])
+        for t in range(PACK):
+            widen(*blocks[2], t)
+        group_pair(1, 0)
+        quant_wd(*blocks[0])
+        group_pair(1, 1)
 
-        def prepare_wd(g, n, widen_on_vector=(), group_on_scalar=()):
-            for t in range(PACK):
-                widen(g, n, t, t in widen_on_vector)
-            for j in range(PACK):
-                scale_group(g, n, j, j in group_on_scalar)
-            quant_wd(g, n)
-
-        def prepare_h(g, on_scalar=()):
-            group_h(g, 0, 0 in on_scalar)
-            group_h(g, 1, 1 in on_scalar)
-            quant_h(g)
-
+        up_matmuls(0)
         for i in range(FT):
             g, s = divmod(i, PACK)
-            up_matmuls(i)
+            if i + 1 < FT:
+                up_matmuls(i + 1)
+            if s == 0:
+                quant_wd(*blocks[1 + g])
+            elif s < 3 and g < FG - 1:
+                group_pair(2 + g, s - 1)
+            elif s < 3:
+                group_h(0, s - 1)
+            elif g == FG - 1:
+                quant_h(0)
             sigmoid(i)
+            widen(*blocks[3 + g], s)
             gate(i)
             if g == FG - 1:
                 shuffle(g, s)
             elif s % 2 == 1:
                 park_store(g, s - 1, s + 1)
-            if i in (7, 11, 13):
-                park_load((7, 11, 13).index(i))
-        prepare_wd(0, 0, (0, 2, 3))
-        for g in range(1, FG):
-            prepare_wd(g, 0)
+            if i in (7, 11, 12):
+                park_load((7, 11, 12).index(i))
+
+        half = T // 2
         for m in range(TT):
             res_turn(m)
+        down_pass(1, 0)
+        group_h(1, 0)
+        group_h(1, 1, "S")
+        for m in range(TT):
             res_copy(m)
-        for g in range(FG):
-            prepare_h(g, HS[g])
-            down_pass(0, g)
-        half = T // 2
+        down_pass(0, 0)
+        group_pair(5, 0)
+        quant_h(1)
+        down_pass(0, 1)
+        down_pass(1, 1)
+        group_pair(5, 1)
+        group_h(2, 0)
+        group_h(2, 1, "S")
+        quant_wd(*blocks[5])
+        group_pair(6, 0)
+        quant_h(2)
+        down_pass(0, 2)
+        widen(*blocks[7], 0)
+        group_h(3, 0)
+        group_h(3, 1, "S")
+        for t in range(1, PACK):
+            widen(*blocks[7], t)
+        group_pair(6, 1)
+        quant_h(3)
+        down_pass(0, 3)
+        quant_wd(*blocks[6])
+        down_pass(1, 2)
+        group_pair(7, 0, "S")
+        group_pair(7, 1, "S")
         for s in range(PACK):
             finish(0, s)
+        group_y(0, 0, "V")
+        quant_wd(*blocks[7])
         for m in range(TT):
             y_turn(0, m)
+        down_pass(1, 3)
+        for m in range(TT):
             y_out(0, m)
-        for g in range(FG):
-            prepare_wd(g, 1, (), WS[g])
-            down_pass(1, g)
-        group_y(0, 0, YV[0])
-        group_y(0, 1, YV[1])
+        group_y(0, 1, "V")
+        finish(1, 0, 0, half)
         quant_y(0)
         scales_out(0, [nc.sync])
-        for h in range(2):
-            for s in range(PACK):
-                finish(1, s, half * h, half * (h + 1))
-            for m in (2 * h, 2 * h + 1):
-                y_turn(1, m)
-                y_out(1, m)
-            group_y(1, h, YV[2 + h])
-            quant_y(1, half * h, half * (h + 1))
+        for s in range(1, PACK):
+            finish(1, s, 0, half)
+        y_turn(1, 0)
+        y_turn(1, 1)
+        for s in range(PACK):
+            finish(1, s, half, T)
+        y_turn(1, 2)
+        y_turn(1, 3)
+        y_out(1, 0)
+        y_out(1, 1)
+        group_y(1, 0, "S")
+        group_y(1, 1, "V")
+        y_out(1, 2, True)
+        y_out(1, 3)
+        quant_y(1, 0, half)
+        quant_y(1, half, T)
         scales_out(1, [nc.sync, nc.scalar])

@@ -24,7 +24,8 @@ DG = D // KP
 FG = F // KP
 FT = F // P
 TT = T // P
-RES_STEP = 9
+ABANK = (0, 1, 6)
+BBANK = (2, 3, 7)
 
 
 def tile_fp4_sigmoid_glu_ffn_b16_kernel(
@@ -50,11 +51,13 @@ def tile_fp4_sigmoid_glu_ffn_b16_kernel(
                 wd_bytes[g, u] = kept("wd_bytes%d_%d" % (g, u), [P, 2 * D], U8)
         x_words = kept("x_words", [P, DG, 2 * T], U8)
         x_scales = kept("x_scales", [P, DG, T], U8)
-        wg_words = [kept("wg_words%d" % g, [P, DG, 2 * KP], U8) for g in range(FG)]
-        wu_words = [kept("wu_words%d" % g, [P, DG, 2 * KP], U8) for g in range(FG)]
+        spans = [(0, KP), (KP, 2 * KP), (2 * KP, F)]
+        wg_words = [kept("wg_words%d" % c, [P, DG, 2 * (f1 - f0)], U8) for c, (f0, f1) in enumerate(spans)]
+        wu_words = [kept("wu_words%d" % c, [P, DG, 2 * (f1 - f0)], U8) for c, (f0, f1) in enumerate(spans)]
         wg_scales = [kept("wg_scales0", [P, DG, KP], U8), kept("wg_scales1", [P, DG, F - KP], U8)]
         wu_scales = [kept("wu_scales0", [P, DG, KP], U8), kept("wu_scales1", [P, DG, F - KP], U8)]
-        table = kept("table", [P, F // P * 8], F32)
+        table = kept("table", [P, F // P], F32)
+        spread = kept("spread", [P, FG, P], F32)
         wd_scale = kept("wd_scale", [P, FG, 8], F32)
         bg_rows = kept("bg_rows", [P, P], BF16)
         bias = kept("bias", [P, FT], F32)
@@ -79,10 +82,10 @@ def tile_fp4_sigmoid_glu_ffn_b16_kernel(
         y_codes = [kept("y_codes%d" % n, [P, T], U32) for n in range(DG)]
         y_mx = [kept("y_mx%d" % n, [P, T], U8) for n in range(DG)]
 
-        def load_words(dst, src, g):
+        def load_words(dst, src, c):
             view = src.bitcast(I32).rearrange("d p w -> p d w")
-            width = dst.shape[2] // 4
-            nc.sync.dma_start(out=dst[:].bitcast(I32), in_=view[:, :, width * g : width * (g + 1)])
+            first = spans[c][0] // 2
+            nc.sync.dma_start(out=dst[:].bitcast(I32), in_=view[:, :, first : first + dst.shape[2] // 4])
 
         def load_scales(dst, src, first=0):
             cols = slice(first // 4, (first + dst.shape[2]) // 4)
@@ -99,13 +102,15 @@ def tile_fp4_sigmoid_glu_ffn_b16_kernel(
 
         nc.vector.memset(warm[:], 0.0)
         nc.scalar.activation(out=warm[:, 4:5], in_=warm[:, 0:1], func=ACT.Sigmoid)
+        nc.vector.memset(table[:], 0.0)
         nc.vector.memset(bg_rows[:], 0.0)
         for plane in (x_scales, wg_scales[0], wu_scales[0], wg_scales[1], wu_scales[1]):
             nc.vector.memset(plane[:].bitcast(I32), 0)
         make_identity(nc, ident[:])
 
         load_wd(0, (0,))
-        nc.sync.dma_start(out=table[:], in_=Wd_scale.rearrange("i j -> (i j)").partition_broadcast(P))
+        with nc.allow_non_contiguous_dma(reason="128 scales, one column of the table to a partition"):
+            nc.sync.dma_start(out=table[0:8, :], in_=Wd_scale.rearrange("i j -> j i"))
         load_wd(0, (1,))
         load_scales(x_scales, XT_scales)
         nc.sync.dma_start(out=bg_rows[0:FT, :], in_=bg.rearrange("(i p) -> i p", p=P))
@@ -116,26 +121,35 @@ def tile_fp4_sigmoid_glu_ffn_b16_kernel(
         load_wd(1, (1,))
         load_words(wu_words[0], Wu_words, 0)
         load_scales(wu_scales[0], Wu_scales)
+        load_wd(2)
         load_scales(wg_scales[1], Wg_scales, KP)
         load_scales(wu_scales[1], Wu_scales, KP)
-        for g in range(1, FG):
-            load_words(wg_words[g], Wg_words, g)
-            load_words(wu_words[g], Wu_words, g)
-            if g + 1 < FG:
-                load_wd(g + 1)
-        nc.sync.dma_start(out=gain_sb[:, :, 0:PACK], in_=gain.rearrange("(n p t) -> p n t", p=P, t=PACK))
-        for m in range(TT):
-            nc.sync.dma_start(out=res_sb[m][:], in_=res[P * m : P * (m + 1), :])
+        load_words(wg_words[1], Wg_words, 1)
+        load_words(wu_words[1], Wu_words, 1)
+        load_wd(3)
+        load_words(wg_words[2], Wg_words, 2)
+        load_words(wu_words[2], Wu_words, 2)
 
-        nc.vector.tensor_copy(out=ident_bf[:], in_=ident[:])
-        by_quadrant = table[:].rearrange("p (g q j) -> p q g j", g=FG, q=4)
+        def load_res():
+            nc.sync.dma_start(out=gain_sb[:, :, 0:PACK], in_=gain.rearrange("(n p t) -> p n t", p=P, t=PACK))
+            for m in range(TT):
+                nc.sync.dma_start(out=res_sb[m][:], in_=res[P * m : P * (m + 1), :])
 
         def pick_scales():
-            for q in range(4):
-                nc.vector.tensor_copy(out=wd_scale[32 * q : 32 * q + 32], in_=by_quadrant[32 * q : 32 * q + 32, q])
+            nc.vector.tensor_copy(
+                out=spread[:].rearrange("j g (q r) -> j (g q) r", q=4),
+                in_=table[:].unsqueeze(2).to_broadcast([P, F // P, 32]),
+            )
+            scale_ps = bank(4, (P, FG, P))
+            for g in range(FG):
+                nc.tensor.transpose(scale_ps[:, g, :], spread[:, g, :], ident[:])
+            return scale_ps
 
-        bias_ps = bank(7, (P, P), BF16)
-        nc.tensor.transpose(bias_ps[:], bg_rows[:], ident_bf[:])
+        def turn_bias():
+            nc.vector.tensor_copy(out=ident_bf[:], in_=ident[:])
+            bias_ps = bank(5, (P, P), BF16)
+            nc.tensor.transpose(bias_ps[:], bg_rows[:], ident_bf[:])
+            return bias_ps
 
         wide = {}
         grouped = {}
@@ -176,19 +190,20 @@ def tile_fp4_sigmoid_glu_ffn_b16_kernel(
         def up_matmuls(i):
             g, s = divmod(i, PACK)
             col = P * i - KP * min(g, 1)
-            for name, words, scales, b in (("a", wg_words, wg_scales, i % 2), ("b", wu_words, wu_scales, 2 + i % 2)):
+            wcol = 2 * (P * i - KP * min(g, 2))
+            for name, words, scales, b in (("a", wg_words, wg_scales, ABANK[i % 3]), ("b", wu_words, wu_scales, BBANK[i % 3])):
                 acc[name, i] = bank(b)
                 for d in range(DG):
                     nc.tensor.matmul_mx(
                         out=acc[name, i][:],
-                        lhsT=words[g][:, d, 2 * P * s : 2 * P * (s + 1)].bitcast(FP4X4),
+                        lhsT=words[min(g, 2)][:, d, wcol : wcol + 2 * P].bitcast(FP4X4),
                         lhsT_scale=scales[min(g, 1)][:, d, col : col + P],
                         rhs=x_words[:, d, :].bitcast(FP4X4), rhs_scale=x_scales[:, d, :],
                         start=(d == 0), stop=(d == DG - 1),
                     )
 
         def sigmoid(i):
-            sig[i] = work.tile([P, T], F32, name="sig", bufs=3)
+            sig[i] = work.tile([P, T], F32, name="sig", bufs=4)
             nc.scalar.activation(out=sig[i][:], in_=acc["a", i][:], func=ACT.Sigmoid, bias=bias[:, i : i + 1])
 
         def gate(i):
@@ -201,9 +216,9 @@ def tile_fp4_sigmoid_glu_ffn_b16_kernel(
             rows = park[KP * g : KP * (g + 1), :].rearrange("(s p) w -> p s w", p=P)
             nc.sync.dma_start(out=rows[:, s0:s1, :], in_=h_nat[g][:, s0:s1, :])
 
-        def park_load(g):
+        def park_load(g, parts=P):
             rows = park[KP * g : KP * (g + 1), :].rearrange("(p t) w -> p t w", t=PACK)
-            nc.sync.dma_start(out=h_back[g][:], in_=rows)
+            nc.sync.dma_start(out=h_back[g][0:parts], in_=rows[0:parts])
 
         def shuffle(g, s):
             for t in range(PACK):
@@ -307,17 +322,19 @@ def tile_fp4_sigmoid_glu_ffn_b16_kernel(
                     out=out_2[n, 4 * q : 4 * q + 4, :].bitcast(I32), in_=y_mx[n][32 * q : 32 * q + 4, :].bitcast(I32)
                 )
 
-        blocks = [(0, 0), (0, 1), (1, 0), (1, 1), (2, 0), (3, 0), (2, 1), (3, 1)]
+        blocks = [(0, 0), (0, 1), (1, 0), (2, 0), (3, 0), (1, 1), (2, 1), (3, 1)]
 
         def group_pair(b, half, on="V"):
             for j in range(2 * half, 2 * half + 2):
                 scale_group(*blocks[b], j, on)
 
-        widen(*blocks[0], 0, True)
+        widen(*blocks[0], 0)
         widen(*blocks[0], 1)
-        pick_scales()
+        scale_ps = pick_scales()
+        bias_ps = turn_bias()
         widen(*blocks[0], 2, True)
         widen(*blocks[0], 3, True)
+        nc.vector.tensor_copy(out=wd_scale[:], in_=scale_ps[:, :, 0:8])
         for t in range(PACK):
             widen(*blocks[1], t)
         group_pair(0, 0)
@@ -330,10 +347,11 @@ def tile_fp4_sigmoid_glu_ffn_b16_kernel(
         group_pair(1, 1)
 
         up_matmuls(0)
+        up_matmuls(1)
         for i in range(FT):
             g, s = divmod(i, PACK)
-            if i + 1 < FT:
-                up_matmuls(i + 1)
+            if i + 2 < FT:
+                up_matmuls(i + 2)
             if s == 0:
                 quant_wd(*blocks[1 + g])
             elif s < 3 and g < FG - 1:
@@ -351,66 +369,70 @@ def tile_fp4_sigmoid_glu_ffn_b16_kernel(
                 park_store(g, s - 1, s + 1)
             if i in (7, 11, 12):
                 park_load((7, 11, 12).index(i))
+            if i == 3:
+                load_res()
 
         half = T // 2
         for m in range(TT):
             res_turn(m)
         down_pass(1, 0)
-        group_h(1, 0)
+        group_h(1, 0, "V")
         group_h(1, 1, "S")
         for m in range(TT):
             res_copy(m)
         down_pass(0, 0)
-        group_pair(5, 0)
+        group_pair(5, 0, "V")
         quant_h(1)
         down_pass(0, 1)
-        down_pass(1, 1)
-        group_pair(5, 1)
-        group_h(2, 0)
+        group_pair(5, 1, "V")
+        group_h(2, 0, "V")
         group_h(2, 1, "S")
         quant_wd(*blocks[5])
-        group_pair(6, 0)
+        down_pass(1, 1)
+        group_h(3, 0, "V")
         quant_h(2)
         down_pass(0, 2)
-        widen(*blocks[7], 0)
-        group_h(3, 0)
         group_h(3, 1, "S")
-        for t in range(1, PACK):
-            widen(*blocks[7], t)
-        group_pair(6, 1)
+        group_pair(6, 0, "V")
         quant_h(3)
         down_pass(0, 3)
-        quant_wd(*blocks[6])
-        down_pass(1, 2)
+        for t in range(PACK):
+            widen(*blocks[7], t)
+        group_pair(6, 1, "V")
         group_pair(7, 0, "S")
         group_pair(7, 1, "S")
         for s in range(PACK):
             finish(0, s)
+        quant_wd(*blocks[6])
+        y_turn(0, 0)
+        y_turn(0, 1)
+        y_turn(0, 2)
+        y_turn(0, 3)
+        down_pass(1, 2)
+        y_out(0, 0)
+        y_out(0, 1)
+        y_out(0, 2)
+        y_out(0, 3)
         group_y(0, 0, "V")
         quant_wd(*blocks[7])
-        for m in range(TT):
-            y_turn(0, m)
         down_pass(1, 3)
-        for m in range(TT):
-            y_out(0, m)
         group_y(0, 1, "V")
-        finish(1, 0, 0, half)
-        quant_y(0)
-        scales_out(0, [nc.sync])
-        for s in range(1, PACK):
+        for s in range(PACK):
             finish(1, s, 0, half)
         y_turn(1, 0)
         y_turn(1, 1)
+        quant_y(0)
+        scales_out(0, [nc.sync])
         for s in range(PACK):
             finish(1, s, half, T)
         y_turn(1, 2)
         y_turn(1, 3)
         y_out(1, 0)
         y_out(1, 1)
-        group_y(1, 0, "S")
-        group_y(1, 1, "V")
-        y_out(1, 2, True)
+        group_y(1, 0, "V")
+        y_out(1, 2)
         y_out(1, 3)
+        group_y(1, 1, "V")
         quant_y(1, 0, half)
         quant_y(1, half, T)
         scales_out(1, [nc.sync, nc.scalar])

@@ -80,7 +80,7 @@ def tile_fp4_sigmoid_glu_ffn_b16_kernel(
         y_t = [kept("y_t%d" % n, [P, PACK, T], F32) for n in range(DG)]
         y_grp = [kept("y_grp%d" % n, [P, T, PACK], BF16) for n in range(DG)]
         y_codes = [kept("y_codes%d" % n, [P, T], U32) for n in range(DG)]
-        y_mx = [kept("y_mx%d" % n, [P, T], U8) for n in range(DG)]
+        y_mx = kept("y_mx", [P, DG, T], U8)
 
         def load_words(dst, src, c):
             view = src.bitcast(I32).rearrange("d p w -> p d w")
@@ -292,7 +292,7 @@ def tile_fp4_sigmoid_glu_ffn_b16_kernel(
             for s in range(PACK):
                 nc.tensor.transpose(y_ps[n, m][:, s, :], y_t[n][:, s, P * m : P * (m + 1)], ident[:])
 
-        def y_out(n, m, on_vector=False):
+        def y_out(n, m, on_vector=False, queue=nc.sync):
             y_sb = work.tile([P, KP], F32, name="y_sb", bufs=8)
             dst = y_sb[:].rearrange("r (p s) -> r p s", s=PACK)
             src = y_ps[n, m][:].rearrange("r s p -> r p s")
@@ -300,7 +300,7 @@ def tile_fp4_sigmoid_glu_ffn_b16_kernel(
                 nc.vector.tensor_copy(out=dst, in_=src)
             else:
                 nc.scalar.copy(out=dst, in_=src)
-            nc.sync.dma_start(out=out_0[P * m : P * (m + 1), KP * n : KP * (n + 1)], in_=y_sb[:])
+            queue.dma_start(out=out_0[P * m : P * (m + 1), KP * n : KP * (n + 1)], in_=y_sb[:])
 
         def group_y(n, half, on="S"):
             cols = slice(T // 2 * half, T // 2 * (half + 1))
@@ -310,16 +310,19 @@ def tile_fp4_sigmoid_glu_ffn_b16_kernel(
 
         def quant_y(n, t0=0, t1=T):
             nc.vector.quantize_mx(
-                out=y_codes[n][:, t0:t1].bitcast(FP8X4), scales=y_mx[n][:, t0:t1],
+                out=y_codes[n][:, t0:t1].bitcast(FP8X4), scales=y_mx[:, n, t0:t1],
                 in_=y_grp[n][:, t0:t1, :].rearrange("p c t -> p (c t)"),
             )
             words = out_1[n].rearrange("p m t -> p (m t)").bitcast(I32)
             nc.sync.dma_start(out=words[:, t0:t1], in_=y_codes[n][:, t0:t1].bitcast(I32))
 
         def scales_out(n, queues):
+            if n == 0:
+                return
             for q in range(4):
                 queues[q % len(queues)].dma_start(
-                    out=out_2[n, 4 * q : 4 * q + 4, :].bitcast(I32), in_=y_mx[n][32 * q : 32 * q + 4, :].bitcast(I32)
+                    out=out_2[:, 4 * q : 4 * q + 4, :].rearrange("n r m -> r n m").bitcast(I32),
+                    in_=y_mx[32 * q : 32 * q + 4].bitcast(I32),
                 )
 
         blocks = [(0, 0), (0, 1), (1, 0), (2, 0), (3, 0), (1, 1), (2, 1), (3, 1)]
@@ -401,21 +404,23 @@ def tile_fp4_sigmoid_glu_ffn_b16_kernel(
         group_pair(6, 1, "V")
         group_pair(7, 0, "S")
         group_pair(7, 1, "S")
-        for s in range(PACK):
-            finish(0, s)
+        finish(0, 0)
         quant_wd(*blocks[6])
+        down_pass(1, 2)
+        finish(0, 1)
+        finish(0, 2)
+        finish(0, 3)
+        quant_wd(*blocks[7])
         y_turn(0, 0)
         y_turn(0, 1)
         y_turn(0, 2)
         y_turn(0, 3)
-        down_pass(1, 2)
+        down_pass(1, 3)
         y_out(0, 0)
         y_out(0, 1)
         y_out(0, 2)
         y_out(0, 3)
         group_y(0, 0, "V")
-        quant_wd(*blocks[7])
-        down_pass(1, 3)
         group_y(0, 1, "V")
         for s in range(PACK):
             finish(1, s, 0, half)
@@ -424,15 +429,17 @@ def tile_fp4_sigmoid_glu_ffn_b16_kernel(
         quant_y(0)
         scales_out(0, [nc.sync])
         for s in range(PACK):
-            finish(1, s, half, T)
+            finish(1, s, half, half + P)
         y_turn(1, 2)
+        for s in range(PACK):
+            finish(1, s, half + P, T)
         y_turn(1, 3)
         y_out(1, 0)
         y_out(1, 1)
         group_y(1, 0, "V")
-        y_out(1, 2)
-        y_out(1, 3)
+        y_out(1, 2, queue=nc.scalar)
+        y_out(1, 3, queue=nc.scalar)
         group_y(1, 1, "V")
         quant_y(1, 0, half)
         quant_y(1, half, T)
-        scales_out(1, [nc.sync, nc.scalar])
+        scales_out(1, [nc.sync])

from contextlib import ExitStack

import concourse.mybir as mybir
from concourse.masks import make_identity

T, D, F = 512, 1024, 2048
FLOPS = 2 * T * D * F * 3

F32 = mybir.dt.float32
BF16 = mybir.dt.bfloat16
I32 = mybir.dt.int32
U32 = mybir.dt.uint32
U8 = mybir.dt.uint8
FP8 = mybir.dt.float8_e4m3fn
FP8X4 = mybir.dt.float8_e4m3fn_x4
FP4X4 = mybir.dt.float4_e2m1fn_x4
ACT = mybir.ActivationFunctionType
ALU = mybir.AluOpType

P = 128
PACK = 4
KP = P * PACK
DG = D // KP
FG = F // KP
FT = F // P
TT = T // P
ABANK = (0, 1, 6)
BBANK = (2, 3, 7)


def tile_fp4_sigmoid_glu_ffn_b16_kernel(
    tc, XT_words, XT_scales, Wg_words, Wg_scales, Wu_words, Wu_scales,
    Wd_bytes, Wd_scale, bg, gain, res, out_0, out_1, out_2,
):
    nc = tc.nc
    with ExitStack() as ctx:
        keep = ctx.enter_context(tc.tile_pool(name="keep", bufs=1))
        work = ctx.enter_context(tc.tile_pool(name="work", bufs=2))
        psum = ctx.enter_context(tc.psum_pool(name="psum", bufs=1))
        ctx.enter_context(tc.manual_schedule())

        def kept(name, shape, dtype):
            return keep.tile(shape, dtype, name=name, align_bytes=64)

        def bank(b, shape=(P, KP), dtype=F32):
            return psum.tile(list(shape), dtype, name="bank%d" % b, tag="bank%d" % b)

        wd_bytes = {}
        for g in range(FG):
            for u in range(2):
                wd_bytes[g, u] = kept("wd_bytes%d_%d" % (g, u), [P, 2 * D], U8)
        x_words = kept("x_words", [P, DG, 2 * T], U8)
        x_scales = kept("x_scales", [P, DG, T], U8)
        spans = [(0, KP), (KP, 2 * KP), (2 * KP, F)]
        wg_words = [kept("wg_words%d" % c, [P, DG, 2 * (f1 - f0)], U8) for c, (f0, f1) in enumerate(spans)]
        wu_words = [kept("wu_words%d" % c, [P, DG, 2 * (f1 - f0)], U8) for c, (f0, f1) in enumerate(spans)]
        wg_scales = [kept("wg_scales0", [P, DG, KP], U8), kept("wg_scales1", [P, DG, F - KP], U8)]
        wu_scales = [kept("wu_scales0", [P, DG, KP], U8), kept("wu_scales1", [P, DG, F - KP], U8)]
        table = kept("table", [P, F // P], F32)
        spread = kept("spread", [P, FG, P], F32)
        wd_scale = kept("wd_scale", [P, FG, 8], F32)
        bg_rows = kept("bg_rows", [P, P], BF16)
        bias = kept("bias", [P, FT], F32)
        gain_sb = kept("gain_sb", [P, DG, 16], BF16)
        ident = kept("ident", [P, P], F32)
        ident_bf = kept("ident_bf", [P, P], BF16)
        warm = kept("warm", [P, 8], F32)
        res_sb = [kept("res_sb%d" % m, [P, D], BF16) for m in range(TT)]
        res_t = kept("res_t", [P, DG, 2, T], F32)
        wd_codes = {}
        wd_mx = {}
        for g in range(FG):
            for n in range(DG):
                wd_codes[g, n] = kept("wd_codes%d_%d" % (g, n), [P, KP], U32)
                wd_mx[g, n] = kept("wd_mx%d_%d" % (g, n), [P, KP], U8)
        h_nat = [kept("h_nat%d" % g, [P, PACK, T], BF16) for g in range(FG)]
        h_back = [kept("h_back%d" % g, [P, PACK, T], BF16) for g in range(FG)]
        h_codes = [kept("h_codes%d" % g, [P, T], U32) for g in range(FG)]
        h_mx = [kept("h_mx%d" % g, [P, T], U8) for g in range(FG)]
        y_t = [kept("y_t%d" % n, [P, PACK, T], F32) for n in range(DG)]
        y_grp = [kept("y_grp%d" % n, [P, T, PACK], BF16) for n in range(DG)]
        y_codes = [kept("y_codes%d" % n, [P, T], U32) for n in range(DG)]
        y_mx = kept("y_mx", [P, DG, T], U8)

        def load_words(dst, src, c):
            view = src.bitcast(I32).rearrange("d p w -> p d w")
            first = spans[c][0] // 2
            nc.sync.dma_start(out=dst[:].bitcast(I32), in_=view[:, :, first : first + dst.shape[2] // 4])

        def load_scales(dst, src, first=0):
            cols = slice(first // 4, (first + dst.shape[2]) // 4)
            for q in range(4):
                nc.sync.dma_start(
                    out=dst[32 * q : 32 * q + 4].bitcast(I32),
                    in_=src.bitcast(I32)[:, 4 * q : 4 * q + 4, cols].rearrange("d r w -> r d w"),
                )

        def load_wd(g, halves=(0, 1)):
            rows = Wd_bytes.rearrange("(g p u e) n -> g u p (e n)", p=P, u=2, e=2)
            for u in halves:
                nc.sync.dma_start(out=wd_bytes[g, u][:], in_=rows[g, u])

        nc.vector.memset(warm[:], 0.0)
        nc.scalar.activation(out=warm[:, 4:5], in_=warm[:, 0:1], func=ACT.Sigmoid)
        nc.vector.memset(table[:], 0.0)
        nc.vector.memset(bg_rows[:], 0.0)
        for plane in (x_scales, wg_scales[0], wu_scales[0], wg_scales[1], wu_scales[1]):
            nc.vector.memset(plane[:].bitcast(I32), 0)
        make_identity(nc, ident[:])

        load_wd(0, (0,))
        with nc.allow_non_contiguous_dma(reason="128 scales, one column of the table to a partition"):
            nc.sync.dma_start(out=table[0:8, :], in_=Wd_scale.rearrange("i j -> j i"))
        load_wd(0, (1,))
        load_scales(x_scales, XT_scales)
        nc.sync.dma_start(out=bg_rows[0:FT, :], in_=bg.rearrange("(i p) -> i p", p=P))
        load_words(x_words, XT_words, 0)
        load_wd(1, (0,))
        load_words(wg_words[0], Wg_words, 0)
        load_scales(wg_scales[0], Wg_scales)
        load_wd(1, (1,))
        load_words(wu_words[0], Wu_words, 0)
        load_scales(wu_scales[0], Wu_scales)
        load_wd(2)
        load_scales(wg_scales[1], Wg_scales, KP)
        load_scales(wu_scales[1], Wu_scales, KP)
        load_words(wg_words[1], Wg_words, 1)
        load_words(wu_words[1], Wu_words, 1)
        load_wd(3)
        load_words(wg_words[2], Wg_words, 2)
        load_words(wu_words[2], Wu_words, 2)

        def load_res():
            nc.sync.dma_start(out=gain_sb[:, :, 0:PACK], in_=gain.rearrange("(n p t) -> p n t", p=P, t=PACK))
            for m in range(TT):
                nc.sync.dma_start(out=res_sb[m][:], in_=res[P * m : P * (m + 1), :])

        def pick_scales():
            nc.vector.tensor_copy(
                out=spread[:].rearrange("j g (q r) -> j (g q) r", q=4),
                in_=table[:].unsqueeze(2).to_broadcast([P, F // P, 32]),
            )
            scale_ps = bank(4, (P, FG, P))
            for g in range(FG):
                nc.tensor.transpose(scale_ps[:, g, :], spread[:, g, :], ident[:])
            return scale_ps

        def turn_bias():
            nc.vector.tensor_copy(out=ident_bf[:], in_=ident[:])
            bias_ps = bank(5, (P, P), BF16)
            nc.tensor.transpose(bias_ps[:], bg_rows[:], ident_bf[:])
            return bias_ps

        wide = {}
        grouped = {}

        def widen(g, n, t, on_vector=False):
            if t == 0:
                wide[g, n] = work.tile([P, PACK, KP], BF16, name="wide", bufs=6, align_bytes=64)
            first = D * (t % 2) + KP * n
            src = wd_bytes[g, t // 2][:, first : first + KP].bitcast(FP8)
            if on_vector:
                nc.vector.tensor_copy(out=wide[g, n][:, t, :], in_=src)
            else:
                nc.scalar.copy(out=wide[g, n][:, t, :], in_=src)

        def scale_group(g, n, j, on="V"):
            if j == 0:
                grouped[g, n] = work.tile([P, KP, PACK], BF16, name="grouped", bufs=4, align_bytes=64)
            dst = grouped[g, n][:].rearrange("p (s m) t -> p m t s", s=PACK)[:, 32 * j : 32 * (j + 1)]
            src = wide[g, n][:, :, P * j : P * (j + 1)].rearrange("p t (m s) -> p m t s", s=PACK)
            col = PACK * n + j
            factor = wd_scale[:, g, col : col + 1]
            if on == "S":
                nc.scalar.activation(out=dst, in_=src, func=ACT.Copy, scale=factor)
            elif on == "G":
                nc.gpsimd.tensor_scalar(out=dst, in0=src, scalar1=factor, scalar2=0.0, op0=ALU.mult, op1=ALU.add)
            else:
                nc.vector.tensor_scalar(out=dst, in0=src, scalar1=factor, scalar2=None, op0=ALU.mult)

        def quant_wd(g, n):
            nc.vector.quantize_mx(
                out=wd_codes[g, n][:].bitcast(FP8X4), scales=wd_mx[g, n][:],
                in_=grouped[g, n][:].rearrange("p c t -> p (c t)"),
            )

        acc = {}
        sig = {}

        def up_matmuls(i):
            g, s = divmod(i, PACK)
            col = P * i - KP * min(g, 1)
            wcol = 2 * (P * i - KP * min(g, 2))
            for name, words, scales, b in (("a", wg_words, wg_scales, ABANK[i % 3]), ("b", wu_words, wu_scales, BBANK[i % 3])):
                acc[name, i] = bank(b)
                for d in range(DG):
                    nc.tensor.matmul_mx(
                        out=acc[name, i][:],
                        lhsT=words[min(g, 2)][:, d, wcol : wcol + 2 * P].bitcast(FP4X4),
                        lhsT_scale=scales[min(g, 1)][:, d, col : col + P],
                        rhs=x_words[:, d, :].bitcast(FP4X4), rhs_scale=x_scales[:, d, :],
                        start=(d == 0), stop=(d == DG - 1),
                    )

        def sigmoid(i):
            sig[i] = work.tile([P, T], F32, name="sig", bufs=4)
            nc.scalar.activation(out=sig[i][:], in_=acc["a", i][:], func=ACT.Sigmoid, bias=bias[:, i : i + 1])

        def gate(i):
            g, s = divmod(i, PACK)
            nc.vector.tensor_tensor(out=h_nat[g][:, s, :], in0=acc["b", i][:], in1=sig[i][:], op=ALU.mult)

        park = out_0.bitcast(BF16).rearrange("r (t w) -> (r t) w", t=PACK)

        def park_store(g, s0, s1):
            rows = park[KP * g : KP * (g + 1), :].rearrange("(s p) w -> p s w", p=P)
            nc.sync.dma_start(out=rows[:, s0:s1, :], in_=h_nat[g][:, s0:s1, :])

        def park_load(g, parts=P):
            rows = park[KP * g : KP * (g + 1), :].rearrange("(p t) w -> p t w", t=PACK)
            nc.sync.dma_start(out=h_back[g][0:parts], in_=rows[0:parts])

        def shuffle(g, s):
            for t in range(PACK):
                nc.sync.dma_start(out=h_back[g][32 * s : 32 * (s + 1), t, :], in_=h_nat[g][t:P:PACK, s, :])

        def move(dst, src, on):
            if on == "S":
                nc.scalar.copy(out=dst, in_=src)
            elif on == "G":
                nc.gpsimd.tensor_scalar(out=dst, in0=src, scalar1=1.0, scalar2=0.0, op0=ALU.mult, op1=ALU.add)
            else:
                nc.vector.tensor_copy(out=dst, in_=src)

        h_grp = {}

        def group_h(g, half, on="V"):
            if half == 0:
                h_grp[g] = work.tile([P, T, PACK], BF16, name="h_grp", bufs=4, align_bytes=64)
            cols = slice(T // 2 * half, T // 2 * (half + 1))
            dst = h_grp[g][:, cols, :].rearrange("p (c i) t -> p c t i", i=4)
            src = h_back[g][:, :, cols].rearrange("p t (c i) -> p c t i", i=4)
            move(dst, src, on)

        def quant_h(g):
            nc.vector.quantize_mx(
                out=h_codes[g][:].bitcast(FP8X4), scales=h_mx[g][:],
                in_=h_grp[g][:].rearrange("p c t -> p (c t)"),
            )

        res_ps = {}

        def res_turn(m):
            res_ps[m] = bank(4 + m, (P, DG, 2, P))
            words = res_sb[m][:].bitcast(F32)
            for n in range(DG):
                for u in range(2):
                    nc.tensor.transpose(res_ps[m][:, n, u, :], words[:, 256 * n + u : 256 * (n + 1) : 2], ident[:])

        def res_copy(m):
            nc.scalar.copy(out=res_t[:, :, :, P * m : P * (m + 1)], in_=res_ps[m][:])

        o_ps = {}

        passes = {0: 0, 1: 0}

        def down_pass(n, g):
            passes[n] = passes[n] + 1
            for s in range(PACK):
                if passes[n] == 1:
                    o_ps[n, s] = bank(4 * (1 - n) + s)
                nc.tensor.matmul_mx(
                    out=o_ps[n, s][:],
                    lhsT=wd_codes[g, n][:, P * s : P * (s + 1)].bitcast(FP8X4),
                    lhsT_scale=wd_mx[g, n][:, P * s : P * (s + 1)],
                    rhs=h_codes[g][:].bitcast(FP8X4), rhs_scale=h_mx[g][:],
                    start=(passes[n] == 1), stop=(passes[n] == FG),
                )

        def finish(n, s, t0=0, t1=T):
            u, e = divmod(s, 2)
            res_cols = res_t[:, n, u, :].bitcast(BF16)[:, 2 * t0 + e : 2 * t1 : 2]
            nc.vector.scalar_tensor_tensor(
                out=y_t[n][:, s, t0:t1], in0=o_ps[n, s][:, t0:t1], scalar=gain_sb[:, n, s : s + 1], in1=res_cols,
                op0=ALU.mult, op1=ALU.add,
            )

        y_ps = {}

        def y_turn(n, m):
            y_ps[n, m] = bank(4 + m, (P, PACK, P))
            for s in range(PACK):
                nc.tensor.transpose(y_ps[n, m][:, s, :], y_t[n][:, s, P * m : P * (m + 1)], ident[:])

        def y_out(n, m, on_vector=False, queue=nc.sync):
            y_sb = work.tile([P, KP], F32, name="y_sb", bufs=8)
            dst = y_sb[:].rearrange("r (p s) -> r p s", s=PACK)
            src = y_ps[n, m][:].rearrange("r s p -> r p s")
            if on_vector:
                nc.vector.tensor_copy(out=dst, in_=src)
            else:
                nc.scalar.copy(out=dst, in_=src)
            queue.dma_start(out=out_0[P * m : P * (m + 1), KP * n : KP * (n + 1)], in_=y_sb[:])

        def group_y(n, half, on="S"):
            cols = slice(T // 2 * half, T // 2 * (half + 1))
            dst = y_grp[n][:, cols, :].rearrange("p (c i) t -> p c t i", i=4)
            src = y_t[n][:, :, cols].rearrange("p t (c i) -> p c t i", i=4)
            move(dst, src, on)

        def quant_y(n, t0=0, t1=T):
            nc.vector.quantize_mx(
                out=y_codes[n][:, t0:t1].bitcast(FP8X4), scales=y_mx[:, n, t0:t1],
                in_=y_grp[n][:, t0:t1, :].rearrange("p c t -> p (c t)"),
            )
            words = out_1[n].rearrange("p m t -> p (m t)").bitcast(I32)
            nc.sync.dma_start(out=words[:, t0:t1], in_=y_codes[n][:, t0:t1].bitcast(I32))

        def scales_out(n, queues):
            if n == 0:
                return
            for q in range(4):
                queues[q % len(queues)].dma_start(
                    out=out_2[:, 4 * q : 4 * q + 4, :].rearrange("n r m -> r n m").bitcast(I32),
                    in_=y_mx[32 * q : 32 * q + 4].bitcast(I32),
                )

        blocks = [(0, 0), (0, 1), (1, 0), (2, 0), (3, 0), (1, 1), (2, 1), (3, 1)]

        def group_pair(b, half, on="V"):
            for j in range(2 * half, 2 * half + 2):
                scale_group(*blocks[b], j, on)

        widen(*blocks[0], 0)
        widen(*blocks[0], 1)
        scale_ps = pick_scales()
        bias_ps = turn_bias()
        widen(*blocks[0], 2, True)
        widen(*blocks[0], 3, True)
        nc.vector.tensor_copy(out=wd_scale[:], in_=scale_ps[:, :, 0:8])
        for t in range(PACK):
            widen(*blocks[1], t)
        group_pair(0, 0)
        group_pair(0, 1)
        nc.scalar.copy(out=bias[:], in_=bias_ps[:, 0:FT])
        for t in range(PACK):
            widen(*blocks[2], t)
        group_pair(1, 0)
        quant_wd(*blocks[0])
        group_pair(1, 1)

        up_matmuls(0)
        up_matmuls(1)
        for i in range(FT):
            g, s = divmod(i, PACK)
            if i + 2 < FT:
                up_matmuls(i + 2)
            if s == 0:
                quant_wd(*blocks[1 + g])
            elif s < 3 and g < FG - 1:
                group_pair(2 + g, s - 1)
            elif s < 3:
                group_h(0, s - 1)
            elif g == FG - 1:
                quant_h(0)
            sigmoid(i)
            widen(*blocks[3 + g], s)
            gate(i)
            if g == FG - 1:
                shuffle(g, s)
            elif s % 2 == 1:
                park_store(g, s - 1, s + 1)
            if i in (7, 11, 12):
                park_load((7, 11, 12).index(i))
            if i == 3:
                load_res()

        half = T // 2
        for m in range(TT):
            res_turn(m)
        down_pass(1, 0)
        group_h(1, 0, "V")
        group_h(1, 1, "S")
        for m in range(TT):
            res_copy(m)
        down_pass(0, 0)
        group_pair(5, 0, "V")
        quant_h(1)
        down_pass(0, 1)
        group_pair(5, 1, "V")
        group_h(2, 0, "V")
        group_h(2, 1, "S")
        quant_wd(*blocks[5])
        down_pass(1, 1)
        group_h(3, 0, "V")
        quant_h(2)
        down_pass(0, 2)
        group_h(3, 1, "S")
        group_pair(6, 0, "V")
        quant_h(3)
        down_pass(0, 3)
        for t in range(PACK):
            widen(*blocks[7], t)
        group_pair(6, 1, "V")
        group_pair(7, 0, "S")
        group_pair(7, 1, "S")
        finish(0, 0)
        quant_wd(*blocks[6])
        down_pass(1, 2)
        finish(0, 1)
        finish(0, 2)
        finish(0, 3)
        quant_wd(*blocks[7])
        y_turn(0, 0)
        y_turn(0, 1)
        y_turn(0, 2)
        y_turn(0, 3)
        down_pass(1, 3)
        y_out(0, 0)
        y_out(0, 1)
        y_out(0, 2)
        y_out(0, 3)
        group_y(0, 0, "V")
        group_y(0, 1, "V")
        for s in range(PACK):
            finish(1, s, 0, half)
        y_turn(1, 0)
        y_turn(1, 1)
        quant_y(0)
        scales_out(0, [nc.sync])
        for s in range(PACK):
            finish(1, s, half, half + P)
        y_turn(1, 2)
        for s in range(PACK):
            finish(1, s, half + P, T)
        y_turn(1, 3)
        y_out(1, 0)
        y_out(1, 1)
        group_y(1, 0, "V")
        y_out(1, 2, queue=nc.scalar)
        y_out(1, 3, queue=nc.scalar)
        group_y(1, 1, "V")
        quant_y(1, 0, half)
        quant_y(1, half, T)
        scales_out(1, [nc.sync])
